import numpy as np
import ml_dtypes


def mxq(x, axis, fmt="e4m3"):
    dtype, down = {"e4m3": (ml_dtypes.float8_e4m3fn, 7), "e5m2": (ml_dtypes.float8_e5m2, 14)}[fmt]
    v = np.moveaxis(np.asarray(x, np.float32).astype(ml_dtypes.bfloat16).astype(np.float64), axis, -1)
    blocks = v.reshape(v.shape[:-1] + (-1, 32))
    amax = np.abs(blocks).max(-1, keepdims=True)
    byte = np.maximum(np.where(amax > 0, np.frexp(amax)[1] - 1 + 127, 0) - down, 1)
    scale = np.exp2(byte - 127.0)
    codes = (blocks / scale).astype(np.float32).astype(dtype).astype(np.float64)
    return np.moveaxis((codes * scale).reshape(v.shape), -1, axis)


WIDE = False


def mx_kscale(k):
    if not WIDE:
        return np.ones(k)
    levels = np.array([10, -10, 5, -5, 0])
    if k % 512:
        return np.exp2(np.random.permutation(np.resize(levels, k // 32))).repeat(32)
    a = np.empty((k // 512, 16))
    for p in range(k // 512):
        a[p, :8] = np.random.permutation(np.resize(levels, 8))
        for g in range(8):
            far = levels[np.abs(levels - a[p, g]) >= 10]
            a[p, g + 8] = far[np.random.randint(len(far))]
    return np.exp2(a.ravel()).repeat(32)


BF16 = ml_dtypes.bfloat16


def bf(x):
    return np.asarray(x, np.float32).astype(BF16)


def f64(x):
    return np.asarray(x).astype(np.float64)


E2M1 = np.array([0.0, 0.5, 1.0, 1.5, 2.0, 3.0, 4.0, 6.0, -0.0, -0.5, -1.0, -1.5, -2.0, -3.0, -4.0, -6.0])


def pack_weight(w, fmt):
    k, n = w.shape
    w = f64(bf(w)).reshape(k // 32, 32, n)
    amax = np.abs(w).max(1)
    if fmt == "e4m3":
        byte = np.frexp(amax)[1] - 1 + 127 - 7
    else:
        mant, ex = np.frexp(amax / 6.0)
        byte = np.where(mant > 0.5, ex, ex - 1) + 127
    byte = np.clip(np.where(amax > 0, byte, 1), 1, 254)
    scaled = (w * np.exp2(127.0 - byte)[:, None, :]).reshape(k, n).astype(np.float32)
    by_word = np.ascontiguousarray(scaled.reshape(k // 512, 128, 4, n).transpose(0, 1, 3, 2))
    if fmt == "e4m3":
        words = by_word.astype(ml_dtypes.float8_e4m3fn).view(np.uint8)
    else:
        c = by_word.astype(ml_dtypes.float4_e2m1fn).view(np.uint8) & 0xF
        words = c[..., 0::2] | (c[..., 1::2] << 4)
    return np.ascontiguousarray(words), np.ascontiguousarray(byte.astype(np.uint8).reshape(k // 512, 16, n))


def unpack_weight(words, scales, fmt):
    g, p, n, _ = words.shape
    if fmt == "e4m3":
        vals = np.ascontiguousarray(words).view(ml_dtypes.float8_e4m3fn).astype(np.float64)
    else:
        nib = np.empty((g, p, n, 4), np.uint8)
        nib[..., 0::2] = words & 0xF
        nib[..., 1::2] = words >> 4
        vals = E2M1[nib]
    vals = vals * np.repeat(np.exp2(scales.astype(np.float64) - 127.0), 8, axis=1)[..., None]
    return vals.transpose(0, 1, 3, 2).reshape(g * 512, n)

E4M3FN = np.array([(-1.0 if i & 128 else 1.0) * ((1.0 + (i & 7) / 8.0) * 2.0 ** (((i >> 3) & 15) - 7) if i & 120 else (i & 7) * 2.0 ** -9) for i in range(256)])


def e4m3fn_bytes(y):
    return np.clip(np.asarray(y, np.float64), -448.0, 448.0).astype(np.float32).astype(ml_dtypes.float8_e4m3fn).view(np.uint8)


def e4m3fn_values(b):
    return E4M3FN[b]


T, N, D, R, O = 1024, 512, 1024, 1024, 1024


def softmax(v):
    e = np.exp(v - v.max(axis=-1, keepdims=True))
    return e / e.sum(axis=-1, keepdims=True)


def expert_coefficients(logits, egain):
    n_experts = logits.shape[-1]
    return np.sqrt(n_experts) * softmax(logits) * egain[None, :]


def draw0():
    sn, sd, t = mx_kscale(N), mx_kscale(D), mx_kscale(R)
    z = bf(np.random.standard_normal((T, D)) * sd)
    logits = bf(np.random.standard_normal((T, N)))
    egain = bf(np.random.standard_normal(N) * sn)
    fa_words, fa_scales = pack_weight(np.random.standard_normal((N, R)) * 0.6 / sn[:, None] * t, "e4m3")
    fb_words, fb_scales = pack_weight(np.random.standard_normal((D, R)) / np.sqrt(D) / sd[:, None], "e4m3")
    bb = bf(np.random.standard_normal(R) * 0.3)
    fc_words, fc_scales = pack_weight(np.random.standard_normal((R, O)) / np.sqrt(R) / t[:, None], "e4m3")
    return {
        "z": z,
        "logits": logits,
        "egain": egain,
        "fa_words": fa_words,
        "fa_scales": fa_scales,
        "fb_words": fb_words,
        "fb_scales": fb_scales,
        "bb": bb,
        "fc_words": fc_words,
        "fc_scales": fc_scales,
    }


def core(z, logits, egain, fa_words, fa_scales, fb_words, fb_scales, bb, fc_words, fc_scales):
    a = expert_coefficients(f64(logits), f64(egain))
    s = mxq(a, 1, "e4m3") @ unpack_weight(fa_words, fa_scales, "e4m3")
    u = (mxq(f64(z), 1, "e4m3") @ unpack_weight(fb_words, fb_scales, "e4m3")) + f64(bb)[None, :]
    h = s * u
    return mxq(h, 1, "e4m3") @ unpack_weight(fc_words, fc_scales, "e4m3")


def setup_inputs():
    drawn = draw0()
    full = np.asarray(drawn['z']).astype(np.float64)
    scale = (np.abs(full).reshape(1024, 8, 128).max(axis=(2,)) / 448.0).astype(np.float32)
    given = {}
    for key, value in drawn.items():
        if key == 'z':
            given['z_bytes'] = e4m3fn_bytes(full / np.repeat(scale.astype(np.float64), 128, axis=1))
            given['z_scale'] = scale
        else:
            given[key] = value
    return given


def reference(z_bytes, z_scale, logits, egain, fa_words, fa_scales, fb_words, fb_scales, bb, fc_words, fc_scales):
    return core(e4m3fn_values(z_bytes) * np.repeat(z_scale.astype(np.float64), 128, axis=1), logits, egain, fa_words, fa_scales, fb_words, fb_scales, bb, fc_words, fc_scales)

@@ -1,0 +1,327 @@
+from contextlib import ExitStack
+
+import concourse.mybir as mybir
+from concourse.masks import make_identity
+
+T, N, D, R, O = 1024, 512, 1024, 1024, 1024
+FLOPS = 2 * T * R * (N + D) + 2 * T * R * O
+
+F32 = mybir.dt.float32
+BF16 = mybir.dt.bfloat16
+I32 = mybir.dt.int32
+U32 = mybir.dt.uint32
+U8 = mybir.dt.uint8
+FP8 = mybir.dt.float8_e4m3fn
+FP8X4 = mybir.dt.float8_e4m3fn_x4
+ACT = mybir.ActivationFunctionType
+ALU = mybir.AluOpType
+AX = mybir.AxisListType
+
+P = 128
+NT = T // P
+MANUAL = False
+
+
+def tile_cpmultilinearmumoe_d1p_kernel(
+    tc, z_bytes, z_scale, logits, egain, fa_words, fa_scales, fb_words, fb_scales, bb, fc_words, fc_scales, out
+):
+    nc = tc.nc
+    with ExitStack() as ctx:
+        keep = ctx.enter_context(tc.tile_pool(name="keep", bufs=1))
+        work = ctx.enter_context(tc.tile_pool(name="work", bufs=3))
+        psum = ctx.enter_context(tc.psum_pool(name="psum", bufs=1))
+        if MANUAL:
+            ctx.enter_context(tc.manual_schedule())
+
+        z_view = z_bytes.rearrange("(p i) k -> p i k", i=NT)
+        l_view = logits.rearrange("(p i) n -> p i n", i=NT)
+        o_view = out.rearrange("(p i) o -> p i o", i=NT)
+
+        chunks = [(0, 1), (1, 2), (2, 4), (4, 6), (6, 8)]
+        zb_tiles = {}
+        l_tiles = {}
+        l_chunks = {}
+
+        def load_tokens(c):
+            i0, i1 = chunks[c]
+            lt = keep.tile([P, i1 - i0, N], BF16, name="logits_%d" % c)
+            nc.sync.dma_start(out=lt[:], in_=l_view[:, i0:i1, :])
+            zt = keep.tile([P, i1 - i0, D], U8, name="zbytes_%d" % c)
+            nc.sync.dma_start(out=zt[:], in_=z_view[:, i0:i1, :])
+            l_chunks[c] = lt
+            for i in range(i0, i1):
+                l_tiles[i] = lt[:, i - i0, :]
+                zb_tiles[i] = zt[:, i - i0, :]
+
+        warm = keep.tile([P, 1], F32, name="warm")
+        nc.vector.memset(warm[:], 0.0)
+        nc.scalar.activation(out=warm[:], in_=warm[:], func=ACT.Exp)
+
+        load_tokens(0)
+        zsc = keep.tile([P, NT * 8], F32, name="zsc")
+        nc.sync.dma_start(out=zsc[:], in_=z_scale.rearrange("(p i) j -> p (i j)", i=NT))
+
+        eg_row = keep.tile([P, N], BF16, name="eg_row")
+        nc.vector.memset(eg_row[:], 0.0)
+        nc.sync.dma_start(out=eg_row[0:1, :], in_=egain.unsqueeze(0))
+        ones = keep.tile([P, P], BF16, name="ones")
+        nc.vector.memset(ones[:], 1.0)
+        bb_raw = keep.tile([P, 2, 4], BF16, name="bb_raw")
+        nc.sync.dma_start(out=bb_raw[:], in_=bb.rearrange("(g p t) -> p g t", g=2, t=4))
+
+        ident = keep.tile([P, P], F32, name="ident")
+        make_identity(nc, ident[:])
+
+        ab_scales = keep.tile([P, R], U8, name="ab_scales", align_bytes=64)
+        c_scales = keep.tile([P, O], U8, name="c_scales", align_bytes=64)
+        nc.vector.memset(ab_scales[:].bitcast(I32), 0)
+        nc.vector.memset(c_scales[:].bitcast(I32), 0)
+        fa_raw = keep.tile([P, R], I32, name="fa_raw")
+        nc.sync.dma_start(out=fa_raw[:], in_=fa_words[0].rearrange("p n t -> p (n t)").bitcast(I32))
+        for q in range(4):
+            nc.scalar.dma_start(out=ab_scales[32 * q : 32 * q + 4, :].bitcast(I32), in_=fa_scales[0, 4 * q : 4 * q + 4, :].bitcast(I32))
+            nc.scalar.dma_start(out=ab_scales[32 * q + 4 : 32 * q + 12, :].bitcast(I32), in_=fb_scales[:, 4 * q : 4 * q + 4, :].bitcast(I32))
+        fb_raw = keep.tile([P, 2, R], I32, name="fb_raw")
+        for g in range(2):
+            nc.sync.dma_start(out=fb_raw[:, g, :], in_=fb_words[g].rearrange("p n t -> p (n t)").bitcast(I32))
+        load_tokens(1)
+        load_tokens(2)
+        for q in range(4):
+            nc.sync.dma_start(out=c_scales[32 * q : 32 * q + 8, :].bitcast(I32), in_=fc_scales[:, 4 * q : 4 * q + 4, :].bitcast(I32))
+        fc_c = keep.tile([P, 2, O], I32, name="fc_c", align_bytes=64)
+        for g in range(2):
+            nc.sync.dma_start(out=fc_c[:, g, :], in_=fc_words[g].rearrange("p n t -> p (n t)").bitcast(I32))
+        load_tokens(3)
+        load_tokens(4)
+
+        bb_sb = keep.tile([P, 8], F32, name="bb_sb")
+        nc.vector.tensor_copy(out=bb_sb[:], in_=bb_raw[:].rearrange("p g t -> p (g t)"))
+
+        eg_ps = psum.tile([P, N], F32, name="o_ps", bufs=2)
+        nc.tensor.matmul(eg_ps[:], lhsT=ones[:], rhs=eg_row[:], start=True, stop=True)
+        eg = keep.tile([P, 2, P, 2], F32, name="eg")
+        nc.scalar.activation(
+            out=eg[:],
+            in_=eg_ps[:].rearrange("p (m u e) -> p u m e", u=2, e=2),
+            func=ACT.Copy,
+            scale=float(N) ** 0.5,
+        )
+
+        fa_c = keep.tile([P, R], I32, name="fa_c", align_bytes=64)
+        fb_c = keep.tile([P, 2, R], I32, name="fb_c", align_bytes=64)
+        ab_s = keep.tile([P, R], U8, name="ab_s", align_bytes=64)
+
+        def permute():
+            nc.vector.tensor_copy(
+                out=fa_c[:].rearrange("p (g t m) -> p g t m", g=2, t=4),
+                in_=fa_raw[:].rearrange("p (g m t) -> p g t m", g=2, t=4),
+            )
+            nc.vector.tensor_copy(
+                out=ab_s[:].rearrange("p (g t m) -> p g t m", g=2, t=4),
+                in_=ab_scales[:].rearrange("p (g m t) -> p g t m", g=2, t=4),
+            )
+            for k in range(2):
+                nc.vector.tensor_copy(
+                    out=fb_c[:, k, :].rearrange("p (g t m) -> p g t m", g=2, t=4),
+                    in_=fb_raw[:, k, :].rearrange("p (g m t) -> p g t m", g=2, t=4),
+                )
+
+        nmax = keep.tile([P, NT], F32, name="nmax")
+        ssum = keep.tile([P, NT], F32, name="ssum")
+        rinv = keep.tile([P, NT], F32, name="rinv")
+        st = {}
+
+        def softmax_max(c):
+            i0, i1 = chunks[c]
+            n = i1 - i0
+            lt = l_chunks[c]
+            if n == 1:
+                nc.vector.tensor_reduce(out=nmax[:, i0:i1], in_=lt[:, 0, :], axis=AX.X, op=ALU.max, negate=True)
+                return
+            m1 = work.tile([P, n, 256], BF16, name="m1")
+            nc.vector.tensor_tensor(out=m1[:], in0=lt[:, :, 0:256], in1=lt[:, :, 256:512], op=ALU.max)
+            m2 = work.tile([P, n, 128], BF16, name="m2")
+            nc.vector.tensor_tensor(out=m2[:], in0=m1[:, :, 0:128], in1=m1[:, :, 128:256], op=ALU.max)
+            nc.vector.tensor_reduce(out=nmax[:, i0:i1], in_=m2[:], axis=AX.X, op=ALU.max, negate=True)
+
+        def softmax_exp(i):
+            e = work.tile([P, N], F32, name="e")
+            nc.scalar.activation(
+                out=e[:], in_=l_tiles[i], func=ACT.Exp, bias=nmax[:, i : i + 1], accum_out=ssum[:, i : i + 1]
+            )
+            st["e", i] = e
+
+        def coefficients(i):
+            nc.vector.reciprocal(out=rinv[:, i : i + 1], in_=ssum[:, i : i + 1])
+            a = work.tile([P, N], BF16, name="a")
+            e = st["e", i][:].rearrange("p (m u e) -> p u m e", u=2, e=2)
+            for u in range(2):
+                nc.vector.scalar_tensor_tensor(
+                    out=a[:, 256 * u : 256 * u + 256].rearrange("p (m e) -> p m e", e=2),
+                    in0=e[:, u],
+                    scalar=rinv[:, i : i + 1],
+                    in1=eg[:, u],
+                    op0=ALU.mult,
+                    op1=ALU.mult,
+                )
+            st["a", i] = a
+
+        def widen(i):
+            z = work.tile([P, 2, 2, P, 2], BF16, name="z")
+            for j in range(8):
+                cols = slice(128 * j, 128 * j + 128)
+                src = zb_tiles[i][:, cols].bitcast(FP8)
+                sc = zsc[:, 8 * i + j : 8 * i + j + 1]
+                g, q = divmod(j, 4)
+                dst = z[:, g, :, 32 * q : 32 * q + 32, :].rearrange("p u m e -> p m u e")
+                nc.vector.tensor_scalar(
+                    out=dst, in0=src.rearrange("p (m u e) -> p m u e", u=2, e=2), scalar1=sc, scalar2=None, op0=ALU.mult
+                )
+            st["z", i] = z
+
+        def transposes(i):
+            zw = st["z", i][:].rearrange("p g u m e -> p (g u m e)").bitcast(F32)
+            z_ps = psum.tile([P, 4, P], F32, name="z_ps")
+            for g in range(2):
+                for u in range(2):
+                    nc.tensor.transpose(z_ps[:, 2 * g + u, :], zw[:, 256 * g + 128 * u : 256 * g + 128 * u + 128], ident[:])
+            aw = st["a", i][:].bitcast(F32)
+            a_ps = psum.tile([P, 2, P], F32, name="a_ps")
+            for u in range(2):
+                nc.tensor.transpose(a_ps[:, u, :], aw[:, 128 * u : 128 * u + 128], ident[:])
+            st["z_ps", i] = z_ps
+            st["a_ps", i] = a_ps
+
+        def evict_tr(i):
+            zt = work.tile([P, 2, P, 4], BF16, name="zt", align_bytes=64)
+            nc.scalar.copy(
+                out=zt[:].rearrange("p g n t -> p (g n t)").bitcast(F32).rearrange("p (g n u) -> p g n u", g=2, u=2),
+                in_=st["z_ps", i][:].rearrange("p (g u) n -> p g n u", g=2),
+            )
+            at = work.tile([P, P, 4], BF16, name="at", align_bytes=64)
+            nc.scalar.copy(
+                out=at[:].rearrange("p n t -> p (n t)").bitcast(F32).rearrange("p (n u) -> p n u", u=2),
+                in_=st["a_ps", i][:].rearrange("p u n -> p n u"),
+            )
+            st["zt", i] = zt
+            st["at", i] = at
+
+        def quantize_za(i):
+            zc = work.tile([P, 2 * P], U32, name="zc", align_bytes=64)
+            zs = work.tile([P, 2 * P], U8, name="zs", align_bytes=64)
+            nc.vector.quantize_mx(
+                out=zc[:].bitcast(FP8X4), scales=zs[:], in_=st["zt", i][:].rearrange("p g n t -> p (g n t)")
+            )
+            ac = work.tile([P, P], U32, name="ac", align_bytes=64)
+            as_ = work.tile([P, P], U8, name="as_", align_bytes=64)
+            nc.vector.quantize_mx(
+                out=ac[:].bitcast(FP8X4), scales=as_[:], in_=st["at", i][:].rearrange("p n t -> p (n t)")
+            )
+            st["q", i] = (zc, zs, ac, as_)
+
+        def project(i, g):
+            zc, zs, ac, as_ = st["q", i]
+            u_ps = psum.tile([P, 4, P], F32, name="u_ps", bufs=2)
+            s_ps = psum.tile([P, 4, P], F32, name="s_ps", bufs=2)
+            for t in range(4):
+                cols = slice(512 * g + 128 * t, 512 * g + 128 * t + 128)
+                for k in range(2):
+                    toks = slice(128 * k, 128 * k + 128)
+                    nc.tensor.matmul_mx(
+                        out=u_ps[:, t, :],
+                        lhsT=fb_c[:, k, cols].bitcast(FP8X4),
+                        lhsT_scale=ab_s[4 + 4 * k : P, cols],
+                        rhs=zc[:, toks].bitcast(FP8X4),
+                        rhs_scale=zs[:, toks],
+                        start=(k == 0),
+                        stop=(k == 1),
+                    )
+            for t in range(4):
+                cols = slice(512 * g + 128 * t, 512 * g + 128 * t + 128)
+                nc.tensor.matmul_mx(
+                    out=s_ps[:, t, :],
+                    lhsT=fa_c[:, cols].bitcast(FP8X4),
+                    lhsT_scale=ab_s[:, cols],
+                    rhs=ac[:].bitcast(FP8X4),
+                    rhs_scale=as_[:],
+                    start=True,
+                    stop=True,
+                )
+            st["su", i, g] = (s_ps, u_ps)
+
+        def bias(i, g):
+            u_sb = work.tile([P, 4, P], F32, name="u_sb")
+            for t in range(4):
+                c = 4 * g + t
+                nc.scalar.activation(
+                    out=u_sb[:, t, :], in_=st["su", i, g][1][:, t, :], func=ACT.Identity, bias=bb_sb[:, c : c + 1]
+                )
+            st["u", i, g] = u_sb
+
+        def product(i, g):
+            if g == 0:
+                st["h", i] = work.tile([P, 2, P, 4], BF16, name="h", align_bytes=64)
+            nc.vector.tensor_tensor(
+                out=st["h", i][:, g],
+                in0=st["su", i, g][0][:].rearrange("p t n -> p n t"),
+                in1=st["u", i, g][:].rearrange("p t n -> p n t"),
+                op=ALU.mult,
+            )
+
+        def quantize_h(i):
+            hc = work.tile([P, 2 * P], U32, name="hc", align_bytes=64)
+            hs = work.tile([P, 2 * P], U8, name="hs", align_bytes=64)
+            nc.vector.quantize_mx(
+                out=hc[:].bitcast(FP8X4), scales=hs[:], in_=st["h", i][:].rearrange("p g n t -> p (g n t)")
+            )
+            st["hq", i] = (hc, hs)
+
+        def output(i):
+            hc, hs = st["hq", i]
+            res = work.tile([P, O], F32, name="res")
+            for half in range(2):
+                oc = slice(512 * half, 512 * half + 512)
+                o_ps = psum.tile([P, 512], F32, name="o_ps", bufs=2)
+                for g in range(2):
+                    toks = slice(128 * g, 128 * g + 128)
+                    nc.tensor.matmul_mx(
+                        out=o_ps[:],
+                        lhsT=hc[:, toks].bitcast(FP8X4),
+                        lhsT_scale=hs[:, toks],
+                        rhs=fc_c[:, g, oc].bitcast(FP8X4),
+                        rhs_scale=c_scales[4 * g : P, oc],
+                        start=(g == 0),
+                        stop=(g == 1),
+                    )
+                nc.scalar.copy(out=res[:, oc], in_=o_ps[:])
+            nc.sync.dma_start(out=o_view[:, i, :], in_=res[:])
+
+        chunk_at = {1: 1, 2: 2, 4: 3, 6: 4}
+        softmax_max(0)
+        for n in range(NT + 2):
+            if 0 <= n - 2 < NT:
+                for g in range(2):
+                    bias(n - 2, g)
+                    product(n - 2, g)
+            if n < NT:
+                softmax_exp(n)
+            if 0 <= n - 1 < NT:
+                transposes(n - 1)
+                evict_tr(n - 1)
+            if 0 <= n - 2 < NT:
+                quantize_h(n - 2)
+            if n < NT:
+                widen(n)
+            if n == 0:
+                permute()
+            if 0 <= n - 1 < NT:
+                quantize_za(n - 1)
+            if n < NT:
+                coefficients(n)
+            if n + 1 in chunk_at:
+                softmax_max(chunk_at[n + 1])
+            if 0 <= n - 2 < NT:
+                output(n - 2)
+            if 0 <= n - 1 < NT:
+                for g in range(2):
+                    project(n - 1, g)

@@ -19,7 +19,7 @@ AX = mybir.AxisListType
 
 P = 128
 NT = T // P
-MANUAL = False
+MANUAL = True
 
 
 def tile_cpmultilinearmumoe_d1p_kernel(
@@ -111,20 +111,23 @@ def tile_cpmultilinearmumoe_d1p_kernel(
         fb_c = keep.tile([P, 2, R], I32, name="fb_c", align_bytes=64)
         ab_s = keep.tile([P, R], U8, name="ab_s", align_bytes=64)
 
-        def permute():
+        def permute_fa():
             nc.vector.tensor_copy(
                 out=fa_c[:].rearrange("p (g t m) -> p g t m", g=2, t=4),
                 in_=fa_raw[:].rearrange("p (g m t) -> p g t m", g=2, t=4),
             )
+
+        def permute_scales():
             nc.vector.tensor_copy(
                 out=ab_s[:].rearrange("p (g t m) -> p g t m", g=2, t=4),
                 in_=ab_scales[:].rearrange("p (g m t) -> p g t m", g=2, t=4),
             )
-            for k in range(2):
-                nc.vector.tensor_copy(
-                    out=fb_c[:, k, :].rearrange("p (g t m) -> p g t m", g=2, t=4),
-                    in_=fb_raw[:, k, :].rearrange("p (g m t) -> p g t m", g=2, t=4),
-                )
+
+        def permute_fb(k):
+            nc.vector.tensor_copy(
+                out=fb_c[:, k, :].rearrange("p (g t m) -> p g t m", g=2, t=4),
+                in_=fb_raw[:, k, :].rearrange("p (g m t) -> p g t m", g=2, t=4),
+            )
 
         nmax = keep.tile([P, NT], F32, name="nmax")
         ssum = keep.tile([P, NT], F32, name="ssum")
@@ -179,50 +182,56 @@ def tile_cpmultilinearmumoe_d1p_kernel(
                 )
             st["z", i] = z
 
-        def transposes(i):
+        def transpose_z(i):
             zw = st["z", i][:].rearrange("p g u m e -> p (g u m e)").bitcast(F32)
             z_ps = psum.tile([P, 4, P], F32, name="z_ps")
             for g in range(2):
                 for u in range(2):
                     nc.tensor.transpose(z_ps[:, 2 * g + u, :], zw[:, 256 * g + 128 * u : 256 * g + 128 * u + 128], ident[:])
+            st["z_ps", i] = z_ps
+
+        def transpose_a(i):
             aw = st["a", i][:].bitcast(F32)
             a_ps = psum.tile([P, 2, P], F32, name="a_ps")
             for u in range(2):
                 nc.tensor.transpose(a_ps[:, u, :], aw[:, 128 * u : 128 * u + 128], ident[:])
-            st["z_ps", i] = z_ps
             st["a_ps", i] = a_ps
 
-        def evict_tr(i):
+        def evict_z(i):
             zt = work.tile([P, 2, P, 4], BF16, name="zt", align_bytes=64)
             nc.scalar.copy(
                 out=zt[:].rearrange("p g n t -> p (g n t)").bitcast(F32).rearrange("p (g n u) -> p g n u", g=2, u=2),
                 in_=st["z_ps", i][:].rearrange("p (g u) n -> p g n u", g=2),
             )
+            st["zt", i] = zt
+
+        def evict_a(i):
             at = work.tile([P, P, 4], BF16, name="at", align_bytes=64)
             nc.scalar.copy(
                 out=at[:].rearrange("p n t -> p (n t)").bitcast(F32).rearrange("p (n u) -> p n u", u=2),
                 in_=st["a_ps", i][:].rearrange("p u n -> p n u"),
             )
-            st["zt", i] = zt
             st["at", i] = at
 
-        def quantize_za(i):
+        def quantize_z(i):
             zc = work.tile([P, 2 * P], U32, name="zc", align_bytes=64)
             zs = work.tile([P, 2 * P], U8, name="zs", align_bytes=64)
             nc.vector.quantize_mx(
                 out=zc[:].bitcast(FP8X4), scales=zs[:], in_=st["zt", i][:].rearrange("p g n t -> p (g n t)")
             )
+            st["zq", i] = (zc, zs)
+
+        def quantize_a(i):
             ac = work.tile([P, P], U32, name="ac", align_bytes=64)
             as_ = work.tile([P, P], U8, name="as_", align_bytes=64)
             nc.vector.quantize_mx(
                 out=ac[:].bitcast(FP8X4), scales=as_[:], in_=st["at", i][:].rearrange("p n t -> p (n t)")
             )
-            st["q", i] = (zc, zs, ac, as_)
+            st["aq", i] = (ac, as_)
 
-        def project(i, g):
-            zc, zs, ac, as_ = st["q", i]
+        def project_z(i, g):
+            zc, zs = st["zq", i]
             u_ps = psum.tile([P, 4, P], F32, name="u_ps", bufs=2)
-            s_ps = psum.tile([P, 4, P], F32, name="s_ps", bufs=2)
             for t in range(4):
                 cols = slice(512 * g + 128 * t, 512 * g + 128 * t + 128)
                 for k in range(2):
@@ -236,6 +245,11 @@ def tile_cpmultilinearmumoe_d1p_kernel(
                         start=(k == 0),
                         stop=(k == 1),
                     )
+            st["u_ps", i, g] = u_ps
+
+        def project_a(i, g):
+            ac, as_ = st["aq", i]
+            s_ps = psum.tile([P, 4, P], F32, name="s_ps", bufs=2)
             for t in range(4):
                 cols = slice(512 * g + 128 * t, 512 * g + 128 * t + 128)
                 nc.tensor.matmul_mx(
@@ -247,14 +261,14 @@ def tile_cpmultilinearmumoe_d1p_kernel(
                     start=True,
                     stop=True,
                 )
-            st["su", i, g] = (s_ps, u_ps)
+            st["s_ps", i, g] = s_ps
 
         def bias(i, g):
             u_sb = work.tile([P, 4, P], F32, name="u_sb")
             for t in range(4):
                 c = 4 * g + t
                 nc.scalar.activation(
-                    out=u_sb[:, t, :], in_=st["su", i, g][1][:, t, :], func=ACT.Identity, bias=bb_sb[:, c : c + 1]
+                    out=u_sb[:, t, :], in_=st["u_ps", i, g][:, t, :], func=ACT.Identity, bias=bb_sb[:, c : c + 1]
                 )
             st["u", i, g] = u_sb
 
@@ -263,7 +277,7 @@ def tile_cpmultilinearmumoe_d1p_kernel(
                 st["h", i] = work.tile([P, 2, P, 4], BF16, name="h", align_bytes=64)
             nc.vector.tensor_tensor(
                 out=st["h", i][:, g],
-                in0=st["su", i, g][0][:].rearrange("p t n -> p n t"),
+                in0=st["s_ps", i, g][:].rearrange("p t n -> p n t"),
                 in1=st["u", i, g][:].rearrange("p t n -> p n t"),
                 op=ALU.mult,
             )
@@ -276,52 +290,70 @@ def tile_cpmultilinearmumoe_d1p_kernel(
             )
             st["hq", i] = (hc, hs)
 
-        def output(i):
+        def output(i, half):
             hc, hs = st["hq", i]
-            res = work.tile([P, O], F32, name="res")
-            for half in range(2):
-                oc = slice(512 * half, 512 * half + 512)
-                o_ps = psum.tile([P, 512], F32, name="o_ps", bufs=2)
-                for g in range(2):
-                    toks = slice(128 * g, 128 * g + 128)
-                    nc.tensor.matmul_mx(
-                        out=o_ps[:],
-                        lhsT=hc[:, toks].bitcast(FP8X4),
-                        lhsT_scale=hs[:, toks],
-                        rhs=fc_c[:, g, oc].bitcast(FP8X4),
-                        rhs_scale=c_scales[4 * g : P, oc],
-                        start=(g == 0),
-                        stop=(g == 1),
-                    )
-                nc.scalar.copy(out=res[:, oc], in_=o_ps[:])
-            nc.sync.dma_start(out=o_view[:, i, :], in_=res[:])
+            oc = slice(512 * half, 512 * half + 512)
+            o_ps = psum.tile([P, 512], F32, name="o_ps", bufs=2)
+            for g in range(2):
+                toks = slice(128 * g, 128 * g + 128)
+                nc.tensor.matmul_mx(
+                    out=o_ps[:],
+                    lhsT=hc[:, toks].bitcast(FP8X4),
+                    lhsT_scale=hs[:, toks],
+                    rhs=fc_c[:, g, oc].bitcast(FP8X4),
+                    rhs_scale=c_scales[4 * g : P, oc],
+                    start=(g == 0),
+                    stop=(g == 1),
+                )
+            st["o_ps", i, half] = o_ps
 
-        chunk_at = {1: 1, 2: 2, 4: 3, 6: 4}
-        softmax_max(0)
-        for n in range(NT + 2):
-            if 0 <= n - 2 < NT:
-                for g in range(2):
-                    bias(n - 2, g)
-                    product(n - 2, g)
-            if n < NT:
-                softmax_exp(n)
-            if 0 <= n - 1 < NT:
-                transposes(n - 1)
-                evict_tr(n - 1)
-            if 0 <= n - 2 < NT:
-                quantize_h(n - 2)
-            if n < NT:
-                widen(n)
-            if n == 0:
-                permute()
-            if 0 <= n - 1 < NT:
-                quantize_za(n - 1)
-            if n < NT:
-                coefficients(n)
-            if n + 1 in chunk_at:
-                softmax_max(chunk_at[n + 1])
-            if 0 <= n - 2 < NT:
-                output(n - 2)
-            if 0 <= n - 1 < NT:
-                for g in range(2):
-                    project(n - 1, g)
+        def result(i, half):
+            if half == 0:
+                st["res", i] = work.tile([P, O], F32, name="res")
+            res = st["res", i]
+            oc = slice(512 * half, 512 * half + 512)
+            nc.scalar.copy(out=res[:, oc], in_=st["o_ps", i, half][:])
+            if i == NT - 1:
+                nc.sync.dma_start(out=o_view[:, i, oc], in_=res[:, oc])
+            elif half == 1:
+                nc.sync.dma_start(out=o_view[:, i, :], in_=res[:])
+
+        chunk_at = {0: 0, 1: 1, 2: 2, 4: 3, 6: 4}
+
+        def stage_max(i):
+            if i in chunk_at:
+                softmax_max(chunk_at[i])
+
+        steps = [
+            (lambda i: evict_a(i), 1),
+            (stage_max, 0),
+            (lambda i: permute_fa() if i == 1 else None, 0),
+            (softmax_exp, 0),
+            (lambda i: project_a(i, 0), 2),
+            (lambda i: bias(i, 0), 2),
+            (quantize_h, 3),
+            (quantize_z, 1),
+            (widen, 0),
+            (lambda i: permute_fb(0) if i == 1 else None, 0),
+            (lambda i: project_a(i, 1), 2),
+            (coefficients, 0),
+            (lambda i: permute_scales() if i == 1 else None, 0),
+            (lambda i: output(i, 0), 3),
+            (lambda i: product(i, 0), 2),
+            (lambda i: output(i, 1), 3),
+            (lambda i: bias(i, 1), 2),
+            (lambda i: product(i, 1), 2),
+            (transpose_z, 0),
+            (transpose_a, 0),
+            (lambda i: result(i, 0), 3),
+            (lambda i: result(i, 1), 3),
+            (lambda i: permute_fb(1) if i == 1 else None, 0),
+            (lambda i: project_z(i, 0), 1),
+            (lambda i: project_z(i, 1), 1),
+            (evict_z, 0),
+            (quantize_a, 1),
+        ]
+        for n in range(NT + 3):
+            for step, offset in steps:
+                if 0 <= n - offset < NT:
+                    step(n - offset)

@@ -57,55 +57,54 @@ def tile_cpmultilinearmumoe_d1p_kernel(
         nc.vector.memset(warm[:], 0.0)
         nc.scalar.activation(out=warm[:], in_=warm[:], func=ACT.Exp)
 
-        load_tokens(0)
-        zsc = keep.tile([P, NT * 8], F32, name="zsc")
-        nc.sync.dma_start(out=zsc[:], in_=z_scale.rearrange("(p i) j -> p (i j)", i=NT))
-
+        ab_scales = keep.tile([P, R], U8, name="ab_scales", align_bytes=64)
+        c_scales = keep.tile([P, O], U8, name="c_scales", align_bytes=64)
         eg_row = keep.tile([P, N], BF16, name="eg_row")
-        nc.vector.memset(eg_row[:], 0.0)
-        nc.sync.dma_start(out=eg_row[0:1, :], in_=egain.unsqueeze(0))
         ones = keep.tile([P, P], BF16, name="ones")
+        nc.vector.memset(eg_row[:], 0.0)
+        nc.vector.memset(ab_scales[:].bitcast(I32), 0)
         nc.vector.memset(ones[:], 1.0)
-        bb_raw = keep.tile([P, 2, 4], BF16, name="bb_raw")
-        nc.sync.dma_start(out=bb_raw[:], in_=bb.rearrange("(g p t) -> p g t", g=2, t=4))
-
+        nc.vector.memset(c_scales[:].bitcast(I32), 0)
         ident = keep.tile([P, P], F32, name="ident")
         make_identity(nc, ident[:])
 
-        ab_scales = keep.tile([P, R], U8, name="ab_scales", align_bytes=64)
-        c_scales = keep.tile([P, O], U8, name="c_scales", align_bytes=64)
-        nc.vector.memset(ab_scales[:].bitcast(I32), 0)
-        nc.vector.memset(c_scales[:].bitcast(I32), 0)
+        zsc = keep.tile([P, NT * 8], F32, name="zsc")
+        bb_raw = keep.tile([P, 2, 4], BF16, name="bb_raw")
         fa_raw = keep.tile([P, R], I32, name="fa_raw")
-        nc.sync.dma_start(out=fa_raw[:], in_=fa_words[0].rearrange("p n t -> p (n t)").bitcast(I32))
-        for q in range(4):
-            nc.scalar.dma_start(out=ab_scales[32 * q : 32 * q + 4, :].bitcast(I32), in_=fa_scales[0, 4 * q : 4 * q + 4, :].bitcast(I32))
-            nc.scalar.dma_start(out=ab_scales[32 * q + 4 : 32 * q + 12, :].bitcast(I32), in_=fb_scales[:, 4 * q : 4 * q + 4, :].bitcast(I32))
         fb_raw = keep.tile([P, 2, R], I32, name="fb_raw")
+        fc_c = keep.tile([P, 2, O], I32, name="fc_c", align_bytes=64)
+
+        load_tokens(0)
+        nc.sync.dma_start(out=zsc[:], in_=z_scale.rearrange("(p i) j -> p (i j)", i=NT))
+        nc.sync.dma_start(out=eg_row[0:1, :], in_=egain.unsqueeze(0))
+        load_tokens(1)
+        for q in range(4):
+            nc.sync.dma_start(out=ab_scales[32 * q : 32 * q + 4, :].bitcast(I32), in_=fa_scales[0, 4 * q : 4 * q + 4, :].bitcast(I32))
+            nc.sync.dma_start(out=ab_scales[32 * q + 4 : 32 * q + 12, :].bitcast(I32), in_=fb_scales[:, 4 * q : 4 * q + 4, :].bitcast(I32))
+        nc.sync.dma_start(out=fa_raw[:], in_=fa_words[0].rearrange("p n t -> p (n t)").bitcast(I32))
         for g in range(2):
             nc.sync.dma_start(out=fb_raw[:, g, :], in_=fb_words[g].rearrange("p n t -> p (n t)").bitcast(I32))
-        load_tokens(1)
+        nc.sync.dma_start(out=bb_raw[:], in_=bb.rearrange("(g p t) -> p g t", g=2, t=4))
         load_tokens(2)
         for q in range(4):
             nc.sync.dma_start(out=c_scales[32 * q : 32 * q + 8, :].bitcast(I32), in_=fc_scales[:, 4 * q : 4 * q + 4, :].bitcast(I32))
-        fc_c = keep.tile([P, 2, O], I32, name="fc_c", align_bytes=64)
         for g in range(2):
             nc.sync.dma_start(out=fc_c[:, g, :], in_=fc_words[g].rearrange("p n t -> p (n t)").bitcast(I32))
         load_tokens(3)
         load_tokens(4)
 
-        bb_sb = keep.tile([P, 8], F32, name="bb_sb")
-        nc.vector.tensor_copy(out=bb_sb[:], in_=bb_raw[:].rearrange("p g t -> p (g t)"))
-
         eg_ps = psum.tile([P, N], F32, name="o_ps", bufs=2)
         nc.tensor.matmul(eg_ps[:], lhsT=ones[:], rhs=eg_row[:], start=True, stop=True)
         eg = keep.tile([P, 2, P, 2], F32, name="eg")
-        nc.scalar.activation(
-            out=eg[:],
-            in_=eg_ps[:].rearrange("p (m u e) -> p u m e", u=2, e=2),
-            func=ACT.Copy,
-            scale=float(N) ** 0.5,
-        )
+
+        def spread_gain():
+            nc.scalar.activation(
+                out=eg[:],
+                in_=eg_ps[:].rearrange("p (m u e) -> p u m e", u=2, e=2),
+                func=ACT.Copy,
+                scale=float(N) ** 0.5,
+            )
+
 
         fa_c = keep.tile([P, R], I32, name="fa_c", align_bytes=64)
         fb_c = keep.tile([P, 2, R], I32, name="fb_c", align_bytes=64)
@@ -266,9 +265,8 @@ def tile_cpmultilinearmumoe_d1p_kernel(
         def bias(i, g):
             u_sb = work.tile([P, 4, P], F32, name="u_sb")
             for t in range(4):
-                c = 4 * g + t
                 nc.scalar.activation(
-                    out=u_sb[:, t, :], in_=st["u_ps", i, g][:, t, :], func=ACT.Identity, bias=bb_sb[:, c : c + 1]
+                    out=u_sb[:, t, :], in_=st["u_ps", i, g][:, t, :], func=ACT.Identity, bias=bb_raw[:, g, t : t + 1]
                 )
             st["u", i, g] = u_sb
 
@@ -276,9 +274,9 @@ def tile_cpmultilinearmumoe_d1p_kernel(
             if g == 0:
                 st["h", i] = work.tile([P, 2, P, 4], BF16, name="h", align_bytes=64)
             nc.vector.tensor_tensor(
-                out=st["h", i][:, g],
-                in0=st["s_ps", i, g][:].rearrange("p t n -> p n t"),
-                in1=st["u", i, g][:].rearrange("p t n -> p n t"),
+                out=st["h", i][:, g].rearrange("p (c j) t -> p c t j", j=2),
+                in0=st["s_ps", i, g][:].rearrange("p t (c j) -> p c t j", j=2),
+                in1=st["u", i, g][:].rearrange("p t (c j) -> p c t j", j=2),
                 op=ALU.mult,
             )
 
@@ -312,6 +310,10 @@ def tile_cpmultilinearmumoe_d1p_kernel(
                 st["res", i] = work.tile([P, O], F32, name="res")
             res = st["res", i]
             oc = slice(512 * half, 512 * half + 512)
+            if i == NT - 1 and half == 1:
+                nc.vector.tensor_copy(out=res[:, oc], in_=st["o_ps", i, half][:])
+                nc.scalar.dma_start(out=o_view[:, i, oc], in_=res[:, oc])
+                return
             nc.scalar.copy(out=res[:, oc], in_=st["o_ps", i, half][:])
             if i == NT - 1:
                 nc.sync.dma_start(out=o_view[:, i, oc], in_=res[:, oc])
@@ -329,6 +331,7 @@ def tile_cpmultilinearmumoe_d1p_kernel(
             (stage_max, 0),
             (lambda i: permute_fa() if i == 1 else None, 0),
             (softmax_exp, 0),
+            (lambda i: spread_gain() if i == 0 else None, 0),
             (lambda i: project_a(i, 0), 2),
             (lambda i: bias(i, 0), 2),
             (quantize_h, 3),

@@ -20,6 +20,7 @@ AX = mybir.AxisListType
 P = 128
 NT = T // P
 MANUAL = True
+LAST = NT - 1
 
 
 def tile_cpmultilinearmumoe_d1p_kernel(
@@ -71,25 +72,26 @@ def tile_cpmultilinearmumoe_d1p_kernel(
         zsc = keep.tile([P, NT * 8], F32, name="zsc")
         bb_raw = keep.tile([P, 2, 4], BF16, name="bb_raw")
         fa_raw = keep.tile([P, R], I32, name="fa_raw")
-        fb_raw = keep.tile([P, 2, R], I32, name="fb_raw")
+        fb_raw = keep.tile([P, 2, 2, R // 2], I32, name="fb_raw")
         fc_c = keep.tile([P, 2, O], I32, name="fc_c", align_bytes=64)
 
         load_tokens(0)
         nc.sync.dma_start(out=zsc[:], in_=z_scale.rearrange("(p i) j -> p (i j)", i=NT))
         nc.sync.dma_start(out=eg_row[0:1, :], in_=egain.unsqueeze(0))
         load_tokens(1)
+        fb_view = fb_words.rearrange("k p n t -> p k (n t)").bitcast(I32)
+        for g in range(2):
+            nc.sync.dma_start(out=fb_raw[:, g], in_=fb_view[:, :, 512 * g : 512 * g + 512])
+        for q in range(4):
+            nc.sync.dma_start(out=ab_scales[32 * q + 4 : 32 * q + 12, :].bitcast(I32), in_=fb_scales[:, 4 * q : 4 * q + 4, :].bitcast(I32))
         for q in range(4):
             nc.sync.dma_start(out=ab_scales[32 * q : 32 * q + 4, :].bitcast(I32), in_=fa_scales[0, 4 * q : 4 * q + 4, :].bitcast(I32))
-            nc.sync.dma_start(out=ab_scales[32 * q + 4 : 32 * q + 12, :].bitcast(I32), in_=fb_scales[:, 4 * q : 4 * q + 4, :].bitcast(I32))
         nc.sync.dma_start(out=fa_raw[:], in_=fa_words[0].rearrange("p n t -> p (n t)").bitcast(I32))
-        for g in range(2):
-            nc.sync.dma_start(out=fb_raw[:, g, :], in_=fb_words[g].rearrange("p n t -> p (n t)").bitcast(I32))
         nc.sync.dma_start(out=bb_raw[:], in_=bb.rearrange("(g p t) -> p g t", g=2, t=4))
         load_tokens(2)
         for q in range(4):
             nc.sync.dma_start(out=c_scales[32 * q : 32 * q + 8, :].bitcast(I32), in_=fc_scales[:, 4 * q : 4 * q + 4, :].bitcast(I32))
-        for g in range(2):
-            nc.sync.dma_start(out=fc_c[:, g, :], in_=fc_words[g].rearrange("p n t -> p (n t)").bitcast(I32))
+        nc.sync.dma_start(out=fc_c[:], in_=fc_words.rearrange("g p n t -> p g (n t)").bitcast(I32))
         load_tokens(3)
         load_tokens(4)
 
@@ -122,10 +124,10 @@ def tile_cpmultilinearmumoe_d1p_kernel(
                 in_=ab_scales[:].rearrange("p (g m t) -> p g t m", g=2, t=4),
             )
 
-        def permute_fb(k):
+        def permute_fb(g):
             nc.vector.tensor_copy(
-                out=fb_c[:, k, :].rearrange("p (g t m) -> p g t m", g=2, t=4),
-                in_=fb_raw[:, k, :].rearrange("p (g m t) -> p g t m", g=2, t=4),
+                out=fb_c[:, :, 512 * g : 512 * g + 512].rearrange("p k (t m) -> p k t m", t=4),
+                in_=fb_raw[:, g].rearrange("p k (m t) -> p k t m", t=4),
             )
 
         nmax = keep.tile([P, NT], F32, name="nmax")
@@ -263,7 +265,7 @@ def tile_cpmultilinearmumoe_d1p_kernel(
             st["s_ps", i, g] = s_ps
 
         def bias(i, g):
-            u_sb = work.tile([P, 4, P], F32, name="u_sb")
+            u_sb = work.tile([P, 4, P], F32, name="u_sb", bufs=4)
             for t in range(4):
                 nc.scalar.activation(
                     out=u_sb[:, t, :], in_=st["u_ps", i, g][:, t, :], func=ACT.Identity, bias=bb_raw[:, g, t : t + 1]
@@ -280,42 +282,46 @@ def tile_cpmultilinearmumoe_d1p_kernel(
                 op=ALU.mult,
             )
 
-        def quantize_h(i):
-            hc = work.tile([P, 2 * P], U32, name="hc", align_bytes=64)
-            hs = work.tile([P, 2 * P], U8, name="hs", align_bytes=64)
+        def quantize_h(i, g0, g1):
+            if g0 == 0:
+                st["hq", i] = (
+                    work.tile([P, 2, P], U32, name="hc", align_bytes=64),
+                    work.tile([P, 2, P], U8, name="hs", align_bytes=64),
+                )
+            hc, hs = st["hq", i]
             nc.vector.quantize_mx(
-                out=hc[:].bitcast(FP8X4), scales=hs[:], in_=st["h", i][:].rearrange("p g n t -> p (g n t)")
+                out=hc[:, g0:g1, :].rearrange("p g n -> p (g n)").bitcast(FP8X4),
+                scales=hs[:, g0:g1, :].rearrange("p g n -> p (g n)"),
+                in_=st["h", i][:, g0:g1].rearrange("p g n t -> p (g n t)"),
             )
-            st["hq", i] = (hc, hs)
 
-        def output(i, half):
+        def output(i, half, g0, g1):
+            if g0 == 0:
+                st["o_ps", i, half] = psum.tile([P, 512], F32, name="o_ps", bufs=2)
             hc, hs = st["hq", i]
             oc = slice(512 * half, 512 * half + 512)
-            o_ps = psum.tile([P, 512], F32, name="o_ps", bufs=2)
-            for g in range(2):
-                toks = slice(128 * g, 128 * g + 128)
+            for g in range(g0, g1):
                 nc.tensor.matmul_mx(
-                    out=o_ps[:],
-                    lhsT=hc[:, toks].bitcast(FP8X4),
-                    lhsT_scale=hs[:, toks],
+                    out=st["o_ps", i, half][:],
+                    lhsT=hc[:, g, :].bitcast(FP8X4),
+                    lhsT_scale=hs[:, g, :],
                     rhs=fc_c[:, g, oc].bitcast(FP8X4),
                     rhs_scale=c_scales[4 * g : P, oc],
                     start=(g == 0),
                     stop=(g == 1),
                 )
-            st["o_ps", i, half] = o_ps
 
         def result(i, half):
             if half == 0:
                 st["res", i] = work.tile([P, O], F32, name="res")
             res = st["res", i]
             oc = slice(512 * half, 512 * half + 512)
-            if i == NT - 1 and half == 1:
+            if i == LAST and half == 1:
                 nc.vector.tensor_copy(out=res[:, oc], in_=st["o_ps", i, half][:])
                 nc.scalar.dma_start(out=o_view[:, i, oc], in_=res[:, oc])
                 return
             nc.scalar.copy(out=res[:, oc], in_=st["o_ps", i, half][:])
-            if i == NT - 1:
+            if i == LAST:
                 nc.sync.dma_start(out=o_view[:, i, oc], in_=res[:, oc])
             elif half == 1:
                 nc.sync.dma_start(out=o_view[:, i, :], in_=res[:])
@@ -326,37 +332,59 @@ def tile_cpmultilinearmumoe_d1p_kernel(
             if i in chunk_at:
                 softmax_max(chunk_at[i])
 
+        def only(i, f):
+            return lambda n: f() if n == i else None
+
+        def quantize_h_early(i):
+            if i == LAST:
+                quantize_h(i, 0, 1)
+
+        def quantize_h_rest(i):
+            quantize_h(i, 1 if i == LAST else 0, 2)
+
+        def output_first(i):
+            if i == LAST:
+                output(i, 0, 0, 1)
+                output(i, 1, 0, 1)
+                output(i, 0, 1, 2)
+            else:
+                output(i, 0, 0, 2)
+
+        def output_second(i):
+            output(i, 1, 1 if i == LAST else 0, 2)
+
         steps = [
-            (lambda i: evict_a(i), 1),
-            (stage_max, 0),
-            (lambda i: permute_fa() if i == 1 else None, 0),
-            (softmax_exp, 0),
-            (lambda i: spread_gain() if i == 0 else None, 0),
-            (lambda i: project_a(i, 0), 2),
-            (lambda i: bias(i, 0), 2),
-            (quantize_h, 3),
-            (quantize_z, 1),
             (widen, 0),
-            (lambda i: permute_fb(0) if i == 1 else None, 0),
-            (lambda i: project_a(i, 1), 2),
-            (coefficients, 0),
-            (lambda i: permute_scales() if i == 1 else None, 0),
-            (lambda i: output(i, 0), 3),
-            (lambda i: product(i, 0), 2),
-            (lambda i: output(i, 1), 3),
+            (lambda i: project_z(i, 1), 2),
+            (evict_z, 1),
+            (lambda i: project_a(i, 1), 3),
+            (only(1, lambda: permute_fb(0)), 0),
+            (output_first, 4),
+            (softmax_exp, 0),
+            (only(0, spread_gain), 0),
+            (lambda i: bias(i, 0), 2),
             (lambda i: bias(i, 1), 2),
-            (lambda i: product(i, 1), 2),
+            (quantize_z, 1),
+            (only(1, lambda: permute_fb(1)), 0),
+            (only(1, permute_scales), 0),
+            (output_second, 4),
+            (lambda i: project_a(i, 0), 2),
+            (only(1, permute_fa), 0),
+            (lambda i: result(i, 0), 4),
+            (stage_max, -1),
+            (lambda i: result(i, 1), 4),
+            (quantize_h_early, 3),
+            (lambda i: product(i, 1), 3),
+            (transpose_a, 1),
+            (coefficients, 0),
             (transpose_z, 0),
-            (transpose_a, 0),
-            (lambda i: result(i, 0), 3),
-            (lambda i: result(i, 1), 3),
-            (lambda i: permute_fb(1) if i == 1 else None, 0),
-            (lambda i: project_z(i, 0), 1),
-            (lambda i: project_z(i, 1), 1),
-            (evict_z, 0),
+            (quantize_h_rest, 3),
+            (lambda i: product(i, 0), 2),
+            (evict_a, 1),
             (quantize_a, 1),
+            (lambda i: project_z(i, 0), 1),
         ]
-        for n in range(NT + 3):
+        for n in range(-1, NT + 4):
             for step, offset in steps:
                 if 0 <= n - offset < NT:
                     step(n - offset)

from contextlib import ExitStack

import concourse.mybir as mybir
from concourse.masks import make_identity

T, N, D, R, O = 1024, 512, 1024, 1024, 1024
FLOPS = 2 * T * R * (N + D) + 2 * T * R * O

F32 = mybir.dt.float32
BF16 = mybir.dt.bfloat16
I32 = mybir.dt.int32
U32 = mybir.dt.uint32
U8 = mybir.dt.uint8
FP8 = mybir.dt.float8_e4m3fn
FP8X4 = mybir.dt.float8_e4m3fn_x4
ACT = mybir.ActivationFunctionType
ALU = mybir.AluOpType
AX = mybir.AxisListType

P = 128
NT = T // P
MANUAL = True
LAST = NT - 1


def tile_cpmultilinearmumoe_d1p_kernel(
    tc, z_bytes, z_scale, logits, egain, fa_words, fa_scales, fb_words, fb_scales, bb, fc_words, fc_scales, out
):
    nc = tc.nc
    with ExitStack() as ctx:
        keep = ctx.enter_context(tc.tile_pool(name="keep", bufs=1))
        work = ctx.enter_context(tc.tile_pool(name="work", bufs=3))
        psum = ctx.enter_context(tc.psum_pool(name="psum", bufs=1))
        if MANUAL:
            ctx.enter_context(tc.manual_schedule())

        z_view = z_bytes.rearrange("(p i) k -> p i k", i=NT)
        l_view = logits.rearrange("(p i) n -> p i n", i=NT)
        o_view = out.rearrange("(p i) o -> p i o", i=NT)

        chunks = [(0, 1), (1, 2), (2, 4), (4, 6), (6, 8)]
        zb_tiles = {}
        l_tiles = {}
        l_chunks = {}

        def load_tokens(c):
            i0, i1 = chunks[c]
            lt = keep.tile([P, i1 - i0, N], BF16, name="logits_%d" % c)
            nc.sync.dma_start(out=lt[:], in_=l_view[:, i0:i1, :])
            zt = keep.tile([P, i1 - i0, D], U8, name="zbytes_%d" % c)
            nc.sync.dma_start(out=zt[:], in_=z_view[:, i0:i1, :])
            l_chunks[c] = lt
            for i in range(i0, i1):
                l_tiles[i] = lt[:, i - i0, :]
                zb_tiles[i] = zt[:, i - i0, :]

        warm = keep.tile([P, 1], F32, name="warm")
        nc.vector.memset(warm[:], 0.0)
        nc.scalar.activation(out=warm[:], in_=warm[:], func=ACT.Exp)

        ab_scales = keep.tile([P, R], U8, name="ab_scales", align_bytes=64)
        c_scales = keep.tile([P, O], U8, name="c_scales", align_bytes=64)
        eg_row = keep.tile([P, N], BF16, name="eg_row")
        ones = keep.tile([P, P], BF16, name="ones")
        nc.vector.memset(eg_row[:], 0.0)
        nc.vector.memset(ab_scales[:].bitcast(I32), 0)
        nc.vector.memset(ones[:], 1.0)
        nc.vector.memset(c_scales[:].bitcast(I32), 0)
        ident = keep.tile([P, P], F32, name="ident")
        make_identity(nc, ident[:])

        zsc = keep.tile([P, NT * 8], F32, name="zsc")
        bb_raw = keep.tile([P, 2, 4], BF16, name="bb_raw")
        fa_raw = keep.tile([P, R], I32, name="fa_raw")
        fb_raw = keep.tile([P, 2, 2, R // 2], I32, name="fb_raw")
        fc_c = keep.tile([P, 2, O], I32, name="fc_c", align_bytes=64)

        load_tokens(0)
        nc.sync.dma_start(out=zsc[:], in_=z_scale.rearrange("(p i) j -> p (i j)", i=NT))
        nc.sync.dma_start(out=eg_row[0:1, :], in_=egain.unsqueeze(0))
        load_tokens(1)
        fb_view = fb_words.rearrange("k p n t -> p k (n t)").bitcast(I32)
        for g in range(2):
            nc.sync.dma_start(out=fb_raw[:, g], in_=fb_view[:, :, 512 * g : 512 * g + 512])
        for q in range(4):
            nc.sync.dma_start(out=ab_scales[32 * q + 4 : 32 * q + 12, :].bitcast(I32), in_=fb_scales[:, 4 * q : 4 * q + 4, :].bitcast(I32))
        for q in range(4):
            nc.sync.dma_start(out=ab_scales[32 * q : 32 * q + 4, :].bitcast(I32), in_=fa_scales[0, 4 * q : 4 * q + 4, :].bitcast(I32))
        nc.sync.dma_start(out=fa_raw[:], in_=fa_words[0].rearrange("p n t -> p (n t)").bitcast(I32))
        nc.sync.dma_start(out=bb_raw[:], in_=bb.rearrange("(g p t) -> p g t", g=2, t=4))
        load_tokens(2)
        for q in range(4):
            nc.sync.dma_start(out=c_scales[32 * q : 32 * q + 8, :].bitcast(I32), in_=fc_scales[:, 4 * q : 4 * q + 4, :].bitcast(I32))
        nc.sync.dma_start(out=fc_c[:], in_=fc_words.rearrange("g p n t -> p g (n t)").bitcast(I32))
        load_tokens(3)
        load_tokens(4)

        eg_ps = psum.tile([P, N], F32, name="o_ps", bufs=2)
        nc.tensor.matmul(eg_ps[:], lhsT=ones[:], rhs=eg_row[:], start=True, stop=True)
        eg = keep.tile([P, 2, P, 2], F32, name="eg")

        def spread_gain():
            nc.scalar.activation(
                out=eg[:],
                in_=eg_ps[:].rearrange("p (m u e) -> p u m e", u=2, e=2),
                func=ACT.Copy,
                scale=float(N) ** 0.5,
            )


        fa_c = keep.tile([P, R], I32, name="fa_c", align_bytes=64)
        fb_c = keep.tile([P, 2, R], I32, name="fb_c", align_bytes=64)
        ab_s = keep.tile([P, R], U8, name="ab_s", align_bytes=64)

        def permute_fa():
            nc.vector.tensor_copy(
                out=fa_c[:].rearrange("p (g t m) -> p g t m", g=2, t=4),
                in_=fa_raw[:].rearrange("p (g m t) -> p g t m", g=2, t=4),
            )

        def permute_scales():
            nc.vector.tensor_copy(
                out=ab_s[:].rearrange("p (g t m) -> p g t m", g=2, t=4),
                in_=ab_scales[:].rearrange("p (g m t) -> p g t m", g=2, t=4),
            )

        def permute_fb(g):
            nc.vector.tensor_copy(
                out=fb_c[:, :, 512 * g : 512 * g + 512].rearrange("p k (t m) -> p k t m", t=4),
                in_=fb_raw[:, g].rearrange("p k (m t) -> p k t m", t=4),
            )

        nmax = keep.tile([P, NT], F32, name="nmax")
        ssum = keep.tile([P, NT], F32, name="ssum")
        rinv = keep.tile([P, NT], F32, name="rinv")
        st = {}

        def softmax_max(c):
            i0, i1 = chunks[c]
            n = i1 - i0
            lt = l_chunks[c]
            if n == 1:
                nc.vector.tensor_reduce(out=nmax[:, i0:i1], in_=lt[:, 0, :], axis=AX.X, op=ALU.max, negate=True)
                return
            m1 = work.tile([P, n, 256], BF16, name="m1")
            nc.vector.tensor_tensor(out=m1[:], in0=lt[:, :, 0:256], in1=lt[:, :, 256:512], op=ALU.max)
            m2 = work.tile([P, n, 128], BF16, name="m2")
            nc.vector.tensor_tensor(out=m2[:], in0=m1[:, :, 0:128], in1=m1[:, :, 128:256], op=ALU.max)
            nc.vector.tensor_reduce(out=nmax[:, i0:i1], in_=m2[:], axis=AX.X, op=ALU.max, negate=True)

        def softmax_exp(i):
            e = work.tile([P, N], F32, name="e")
            nc.scalar.activation(
                out=e[:], in_=l_tiles[i], func=ACT.Exp, bias=nmax[:, i : i + 1], accum_out=ssum[:, i : i + 1]
            )
            st["e", i] = e

        def coefficients(i):
            nc.vector.reciprocal(out=rinv[:, i : i + 1], in_=ssum[:, i : i + 1])
            a = work.tile([P, N], BF16, name="a")
            e = st["e", i][:].rearrange("p (m u e) -> p u m e", u=2, e=2)
            for u in range(2):
                nc.vector.scalar_tensor_tensor(
                    out=a[:, 256 * u : 256 * u + 256].rearrange("p (m e) -> p m e", e=2),
                    in0=e[:, u],
                    scalar=rinv[:, i : i + 1],
                    in1=eg[:, u],
                    op0=ALU.mult,
                    op1=ALU.mult,
                )
            st["a", i] = a

        def widen(i):
            z = work.tile([P, 2, 2, P, 2], BF16, name="z")
            for j in range(8):
                cols = slice(128 * j, 128 * j + 128)
                src = zb_tiles[i][:, cols].bitcast(FP8)
                sc = zsc[:, 8 * i + j : 8 * i + j + 1]
                g, q = divmod(j, 4)
                dst = z[:, g, :, 32 * q : 32 * q + 32, :].rearrange("p u m e -> p m u e")
                nc.vector.tensor_scalar(
                    out=dst, in0=src.rearrange("p (m u e) -> p m u e", u=2, e=2), scalar1=sc, scalar2=None, op0=ALU.mult
                )
            st["z", i] = z

        def transpose_z(i):
            zw = st["z", i][:].rearrange("p g u m e -> p (g u m e)").bitcast(F32)
            z_ps = psum.tile([P, 4, P], F32, name="z_ps")
            for g in range(2):
                for u in range(2):
                    nc.tensor.transpose(z_ps[:, 2 * g + u, :], zw[:, 256 * g + 128 * u : 256 * g + 128 * u + 128], ident[:])
            st["z_ps", i] = z_ps

        def transpose_a(i):
            aw = st["a", i][:].bitcast(F32)
            a_ps = psum.tile([P, 2, P], F32, name="a_ps")
            for u in range(2):
                nc.tensor.transpose(a_ps[:, u, :], aw[:, 128 * u : 128 * u + 128], ident[:])
            st["a_ps", i] = a_ps

        def evict_z(i):
            zt = work.tile([P, 2, P, 4], BF16, name="zt", align_bytes=64)
            nc.scalar.copy(
                out=zt[:].rearrange("p g n t -> p (g n t)").bitcast(F32).rearrange("p (g n u) -> p g n u", g=2, u=2),
                in_=st["z_ps", i][:].rearrange("p (g u) n -> p g n u", g=2),
            )
            st["zt", i] = zt

        def evict_a(i):
            at = work.tile([P, P, 4], BF16, name="at", align_bytes=64)
            nc.scalar.copy(
                out=at[:].rearrange("p n t -> p (n t)").bitcast(F32).rearrange("p (n u) -> p n u", u=2),
                in_=st["a_ps", i][:].rearrange("p u n -> p n u"),
            )
            st["at", i] = at

        def quantize_z(i):
            zc = work.tile([P, 2 * P], U32, name="zc", align_bytes=64)
            zs = work.tile([P, 2 * P], U8, name="zs", align_bytes=64)
            nc.vector.quantize_mx(
                out=zc[:].bitcast(FP8X4), scales=zs[:], in_=st["zt", i][:].rearrange("p g n t -> p (g n t)")
            )
            st["zq", i] = (zc, zs)

        def quantize_a(i):
            ac = work.tile([P, P], U32, name="ac", align_bytes=64)
            as_ = work.tile([P, P], U8, name="as_", align_bytes=64)
            nc.vector.quantize_mx(
                out=ac[:].bitcast(FP8X4), scales=as_[:], in_=st["at", i][:].rearrange("p n t -> p (n t)")
            )
            st["aq", i] = (ac, as_)

        def project_z(i, g):
            zc, zs = st["zq", i]
            u_ps = psum.tile([P, 4, P], F32, name="u_ps", bufs=2)
            for t in range(4):
                cols = slice(512 * g + 128 * t, 512 * g + 128 * t + 128)
                for k in range(2):
                    toks = slice(128 * k, 128 * k + 128)
                    nc.tensor.matmul_mx(
                        out=u_ps[:, t, :],
                        lhsT=fb_c[:, k, cols].bitcast(FP8X4),
                        lhsT_scale=ab_s[4 + 4 * k : P, cols],
                        rhs=zc[:, toks].bitcast(FP8X4),
                        rhs_scale=zs[:, toks],
                        start=(k == 0),
                        stop=(k == 1),
                    )
            st["u_ps", i, g] = u_ps

        def project_a(i, g):
            ac, as_ = st["aq", i]
            s_ps = psum.tile([P, 4, P], F32, name="s_ps", bufs=2)
            for t in range(4):
                cols = slice(512 * g + 128 * t, 512 * g + 128 * t + 128)
                nc.tensor.matmul_mx(
                    out=s_ps[:, t, :],
                    lhsT=fa_c[:, cols].bitcast(FP8X4),
                    lhsT_scale=ab_s[:, cols],
                    rhs=ac[:].bitcast(FP8X4),
                    rhs_scale=as_[:],
                    start=True,
                    stop=True,
                )
            st["s_ps", i, g] = s_ps

        def bias(i, g):
            u_sb = work.tile([P, 4, P], F32, name="u_sb", bufs=4)
            for t in range(4):
                nc.scalar.activation(
                    out=u_sb[:, t, :], in_=st["u_ps", i, g][:, t, :], func=ACT.Identity, bias=bb_raw[:, g, t : t + 1]
                )
            st["u", i, g] = u_sb

        def product(i, g):
            if g == 0:
                st["h", i] = work.tile([P, 2, P, 4], BF16, name="h", align_bytes=64)
            nc.vector.tensor_tensor(
                out=st["h", i][:, g].rearrange("p (c j) t -> p c t j", j=2),
                in0=st["s_ps", i, g][:].rearrange("p t (c j) -> p c t j", j=2),
                in1=st["u", i, g][:].rearrange("p t (c j) -> p c t j", j=2),
                op=ALU.mult,
            )

        def quantize_h(i, g0, g1):
            if g0 == 0:
                st["hq", i] = (
                    work.tile([P, 2, P], U32, name="hc", align_bytes=64),
                    work.tile([P, 2, P], U8, name="hs", align_bytes=64),
                )
            hc, hs = st["hq", i]
            nc.vector.quantize_mx(
                out=hc[:, g0:g1, :].rearrange("p g n -> p (g n)").bitcast(FP8X4),
                scales=hs[:, g0:g1, :].rearrange("p g n -> p (g n)"),
                in_=st["h", i][:, g0:g1].rearrange("p g n t -> p (g n t)"),
            )

        def output(i, half, g0, g1):
            if g0 == 0:
                st["o_ps", i, half] = psum.tile([P, 512], F32, name="o_ps", bufs=2)
            hc, hs = st["hq", i]
            oc = slice(512 * half, 512 * half + 512)
            for g in range(g0, g1):
                nc.tensor.matmul_mx(
                    out=st["o_ps", i, half][:],
                    lhsT=hc[:, g, :].bitcast(FP8X4),
                    lhsT_scale=hs[:, g, :],
                    rhs=fc_c[:, g, oc].bitcast(FP8X4),
                    rhs_scale=c_scales[4 * g : P, oc],
                    start=(g == 0),
                    stop=(g == 1),
                )

        def result(i, half):
            if half == 0:
                st["res", i] = work.tile([P, O], F32, name="res")
            res = st["res", i]
            oc = slice(512 * half, 512 * half + 512)
            if i == LAST and half == 1:
                nc.vector.tensor_copy(out=res[:, oc], in_=st["o_ps", i, half][:])
                nc.scalar.dma_start(out=o_view[:, i, oc], in_=res[:, oc])
                return
            nc.scalar.copy(out=res[:, oc], in_=st["o_ps", i, half][:])
            if i == LAST:
                nc.sync.dma_start(out=o_view[:, i, oc], in_=res[:, oc])
            elif half == 1:
                nc.sync.dma_start(out=o_view[:, i, :], in_=res[:])

        chunk_at = {0: 0, 1: 1, 2: 2, 4: 3, 6: 4}

        def stage_max(i):
            if i in chunk_at:
                softmax_max(chunk_at[i])

        def only(i, f):
            return lambda n: f() if n == i else None

        def quantize_h_early(i):
            if i == LAST:
                quantize_h(i, 0, 1)

        def quantize_h_rest(i):
            quantize_h(i, 1 if i == LAST else 0, 2)

        def output_first(i):
            if i == LAST:
                output(i, 0, 0, 1)
                output(i, 1, 0, 1)
                output(i, 0, 1, 2)
            else:
                output(i, 0, 0, 2)

        def output_second(i):
            output(i, 1, 1 if i == LAST else 0, 2)

        steps = [
            (widen, 0),
            (lambda i: project_z(i, 1), 2),
            (evict_z, 1),
            (lambda i: project_a(i, 1), 3),
            (only(1, lambda: permute_fb(0)), 0),
            (output_first, 4),
            (softmax_exp, 0),
            (only(0, spread_gain), 0),
            (lambda i: bias(i, 0), 2),
            (lambda i: bias(i, 1), 2),
            (quantize_z, 1),
            (only(1, lambda: permute_fb(1)), 0),
            (only(1, permute_scales), 0),
            (output_second, 4),
            (lambda i: project_a(i, 0), 2),
            (only(1, permute_fa), 0),
            (lambda i: result(i, 0), 4),
            (stage_max, -1),
            (lambda i: result(i, 1), 4),
            (quantize_h_early, 3),
            (lambda i: product(i, 1), 3),
            (transpose_a, 1),
            (coefficients, 0),
            (transpose_z, 0),
            (quantize_h_rest, 3),
            (lambda i: product(i, 0), 2),
            (evict_a, 1),
            (quantize_a, 1),
            (lambda i: project_z(i, 0), 1),
        ]
        for n in range(-1, NT + 4):
            for step, offset in steps:
                if 0 <= n - offset < NT:
                    step(n - offset)
